import numpy as np
import ml_dtypes


def mxq(x, axis, fmt="e4m3"):
    dtype, down = {"e4m3": (ml_dtypes.float8_e4m3fn, 7), "e5m2": (ml_dtypes.float8_e5m2, 14)}[fmt]
    v = np.moveaxis(np.asarray(x, np.float32).astype(ml_dtypes.bfloat16).astype(np.float64), axis, -1)
    blocks = v.reshape(v.shape[:-1] + (-1, 32))
    amax = np.abs(blocks).max(-1, keepdims=True)
    byte = np.maximum(np.where(amax > 0, np.frexp(amax)[1] - 1 + 127, 0) - down, 1)
    scale = np.exp2(byte - 127.0)
    codes = (blocks / scale).astype(np.float32).astype(dtype).astype(np.float64)
    return np.moveaxis((codes * scale).reshape(v.shape), -1, axis)


WIDE = False


def mx_kscale(k):
    if not WIDE:
        return np.ones(k)
    levels = np.array([10, -10, 5, -5, 0])
    if k % 512:
        return np.exp2(np.random.permutation(np.resize(levels, k // 32))).repeat(32)
    a = np.empty((k // 512, 16))
    for p in range(k // 512):
        a[p, :8] = np.random.permutation(np.resize(levels, 8))
        for g in range(8):
            far = levels[np.abs(levels - a[p, g]) >= 10]
            a[p, g + 8] = far[np.random.randint(len(far))]
    return np.exp2(a.ravel()).repeat(32)


def f64(x):
    return np.asarray(x).astype(np.float64)


def striped(idx):
    return np.tile(idx.reshape(-1, 16).T, (8, 1)).astype(np.uint16)


def unstriped(offs):
    return offs[:16].T.reshape(-1).astype(np.int64)


K, T, D, S, V, N = 1024, 512, 8, 2048, 256, 256


def setup_inputs():
    n = np.random.standard_normal
    s = mx_kscale(K)[:, None]
    return {
        "xT": (n((K, T)) * s).astype(np.float32),
        "w": (n((K, N)) / np.sqrt(K) / s).astype(np.float32),
        "gate": np.tile(np.random.uniform(0.2, 1.0, (D, 1, V)) / np.sqrt(D), (1, N, 1)).astype(np.float32),
        "pos1": striped(np.random.permutation(T)[:V]),
        "pos2": striped(np.random.permutation(T)[:V]),
        "pos3": striped(np.random.permutation(T)[:V]),
        "pos4": striped(np.random.permutation(T)[:V]),
        "pos5": striped(np.random.permutation(T)[:V]),
        "pos6": striped(np.random.permutation(T)[:V]),
        "pos7": striped(np.random.permutation(T)[:V]),
        "pos8": striped(np.random.permutation(T)[:V]),
    }


def reference(xT, w, gate, pos1, pos2, pos3, pos4, pos5, pos6, pos7, pos8):
    y = mxq(f64(w), 0, "e4m3").T @ mxq(f64(xT), 0, "e4m3")
    return sum(f64(gate[d]) * y[:, unstriped(p)] for d, p in enumerate((pos1, pos2, pos3, pos4, pos5, pos6, pos7, pos8)))

@@ -1,0 +1,178 @@
+import concourse.mybir as mybir
+from contextlib import ExitStack
+
+K, T, N, D, V = 1024, 512, 256, 8, 256
+P, PACK = 128, 4
+PASSES = K // (P * PACK)
+FLOPS = 2 * K * T * N + 2 * D * N * V
+
+F32 = mybir.dt.float32
+BF16 = mybir.dt.bfloat16
+U32 = mybir.dt.uint32
+U16 = mybir.dt.uint16
+U8 = mybir.dt.uint8
+FP8X4 = mybir.dt.float8_e4m3fn_x4
+MULT = mybir.AluOpType.mult
+
+
+def tile_picked_agg_lin_none_sub_l_kernel(
+    tc, xT, w, gate, pos1, pos2, pos3, pos4, pos5, pos6, pos7, pos8, out
+):
+    nc = tc.nc
+    lists = (pos1, pos2, pos3, pos4, pos5, pos6, pos7, pos8)
+    with ExitStack() as ctx:
+        keep = ctx.enter_context(tc.tile_pool(name="keep", bufs=1))
+        psum = ctx.enter_context(tc.psum_pool(name="psum", bufs=1))
+
+        w_view = w.rearrange("(c p j) n -> p c j n", c=PASSES, j=PACK)
+        x_view = xT.rearrange("(c p j) t -> p c j t", c=PASSES, j=PACK)
+        w_raw = [[], []]
+
+        def load_w(b):
+            for c in range(PASSES):
+                raw = keep.tile([P, PACK, P], F32, name=f"w_raw{b}_{c}")
+                nc.sync.dma_start(out=raw[:], in_=w_view[:, c, :, b * P : (b + 1) * P])
+                w_raw[b].append(raw)
+
+        x_raw = []
+
+        def load_x(c, a, z):
+            raw = keep.tile([P, PACK, z - a], F32, name=f"x_raw{c}_{a}")
+            nc.sync.dma_start(out=raw[:], in_=x_view[:, c, :, a:z])
+            x_raw.append((c, a, raw))
+
+        load_w(0)
+        load_x(0, 0, T)
+        load_x(1, 0, 384)
+        load_x(1, 384, T)
+
+        gate_view = gate.rearrange("d (b p) v -> p b d v", p=P)
+        gates = [[], []]
+        offs = []
+
+        def load_gate(b, pair):
+            g = keep.tile([P, 2, V], F32, name=f"gate{b}_{pair}")
+            nc.sync.dma_start(out=g[:], in_=gate_view[:, b, 2 * pair : 2 * pair + 2])
+            gates[b].append(g)
+
+        def load_list():
+            d = len(offs)
+            o = keep.tile([P, V // 16], U16, name=f"offs{d}")
+            nc.sync.dma_start(o[:], lists[d])
+            offs.append(o)
+
+        for pair in range(D // 2):
+            load_list()
+            load_gate(0, pair)
+            load_list()
+            if pair == 1:
+                load_w(1)
+        for pair in range(D // 2):
+            load_gate(1, pair)
+
+        def interleave(dst, src, v_cols):
+            cols = dst.shape[1]
+            if v_cols > 0:
+                nc.vector.tensor_copy(out=dst[:, 0:v_cols, :], in_=src[:, :, 0:v_cols].rearrange("p j w -> p w j"))
+            if v_cols < cols:
+                nc.scalar.copy(out=dst[:, v_cols:cols, :], in_=src[:, :, v_cols:cols].rearrange("p j w -> p w j"))
+
+        def quantise(codes, scales, grouped):
+            nc.vector.quantize_mx(
+                out=codes.bitcast(FP8X4), scales=scales, in_=grouped.rearrange("p n j -> p (n j)")
+            )
+
+        w_codes = [keep.tile([P, PASSES, P], U32, name=f"w_codes{b}", align_bytes=64) for b in range(2)]
+        w_scales = [keep.tile([P, PASSES, P], U8, name=f"w_scales{b}", align_bytes=64) for b in range(2)]
+        w_grp = [keep.tile([P, PASSES * P, PACK], BF16, name=f"w_grp{b}", align_bytes=64) for b in range(2)]
+        x_codes = [keep.tile([P, T], U32, name=f"x_codes{c}", align_bytes=64) for c in range(PASSES)]
+        x_scales = [keep.tile([P, T], U8, name=f"x_scales{c}", align_bytes=64) for c in range(PASSES)]
+        x_grp = [keep.tile([P, T, PACK], BF16, name=f"x_grp{c}", align_bytes=64) for c in range(PASSES)]
+
+        def prepare_w(b, v_cols):
+            for c in range(PASSES):
+                interleave(w_grp[b][:, c * P : (c + 1) * P, :], w_raw[b][c][:], v_cols)
+            quantise(
+                w_codes[b][:].rearrange("p c n -> p (c n)"), w_scales[b][:].rearrange("p c n -> p (c n)"), w_grp[b][:]
+            )
+
+        def multiply(acc, b, c, a, z):
+            nc.tensor.matmul_mx(
+                out=acc[:],
+                lhsT=w_codes[b][:, c, :].bitcast(FP8X4),
+                lhsT_scale=w_scales[b][:, c, :],
+                rhs=x_codes[c][:, a:z].bitcast(FP8X4),
+                rhs_scale=x_scales[c][:, a:z],
+                start=(c == 0),
+                stop=(c == PASSES - 1),
+            )
+
+        def prepare_x(c, a, z, raw, first, v_cols):
+            interleave(x_grp[c][:, a:z, :], raw[:, :, a - first : z - first], v_cols)
+            quantise(x_codes[c][:, a:z], x_scales[c][:, a:z], x_grp[c][:, a:z, :])
+
+        prepare_w(0, 80)
+        prepare_x(0, 0, T, x_raw[0][2], 0, 320)
+        spans = ((0, 256), (256, 384), (384, 512))
+        acc0 = [psum.tile([P, z - a], F32, name=f"acc0_{a}") for a, z in spans]
+        acc1 = psum.tile([P, T], F32, name="acc1")
+        for i, (a, z) in enumerate(spans):
+            multiply(acc0[i], 0, 0, a, z)
+
+        y = [keep.tile([P, T], F32, name=f"y{b}") for b in range(2)]
+        for i, (a, z) in enumerate(spans):
+            c_in, first, raw = x_raw[1] if z <= 384 else x_raw[2]
+            prepare_x(1, a, z, raw, first, (z - a) * 5 // 8)
+            multiply(acc0[i], 0, 1, a, z)
+            nc.scalar.copy(out=y[0][:, a:z], in_=acc0[i][:])
+
+        z_t = [keep.tile([P, D, V], F32, name=f"z{b}") for b in range(2)]
+
+        def gather(b, d):
+            nc.vector.tensor_tensor(
+                z_t[b][:, d, :], y[b][:].indirect(offs[d][:]), gates[b][d // 2][:, d % 2, :], MULT
+            )
+
+        s0 = [keep.tile([P, 2, V], F32, name=f"s0_{i}") for i in range(3)]
+        o0 = keep.tile([P, V], F32, name="o0")
+        for d in range(5):
+            gather(0, d)
+        nc.vector.tensor_add(s0[0][:], z_t[0][:, 0:2], z_t[0][:, 2:4])
+        gather(0, 5)
+        prepare_w(1, 0)
+        for c in range(PASSES):
+            multiply(acc1, 1, c, 0, T)
+        nc.scalar.copy(out=y[1][:], in_=acc1[:])
+        gather(0, 6)
+        nc.vector.tensor_add(s0[1][:], s0[0][:], z_t[0][:, 4:6])
+        gather(0, 7)
+        gather(1, 0)
+        nc.vector.tensor_add(s0[2][:], s0[1][:], z_t[0][:, 6:8])
+        gather(1, 1)
+        nc.vector.tensor_add(o0[:], s0[2][:, 0], s0[2][:, 1])
+        nc.sync.dma_start(out=out[0:P, :], in_=o0[:])
+
+        s1 = keep.tile([P, 2, V], F32, name="s1")
+        t1 = keep.tile([P, V], F32, name="t1")
+        u1 = keep.tile([P, V], F32, name="u1")
+        q1 = keep.tile([P, V], F32, name="q1")
+        v1 = keep.tile([P, V], F32, name="v1")
+        for d in range(2, 5):
+            gather(1, d)
+        nc.vector.tensor_add(s1[:], z_t[1][:, 0:2], z_t[1][:, 2:4])
+        gather(1, 5)
+        nc.vector.tensor_add(t1[:], s1[:, 0], s1[:, 1])
+        gather(1, 6)
+        nc.vector.tensor_add(u1[:], z_t[1][:, 4], z_t[1][:, 5])
+        nc.vector.tensor_add(q1[:], t1[:], z_t[1][:, 6])
+        halves = [(0, V // 2), (V // 2, V)]
+        for i, (a, z) in enumerate(halves):
+            nc.vector.tensor_tensor(
+                z_t[1][:, 7, a:z], y[1][:].indirect(offs[7][:, a // 16 : z // 16]), gates[1][3][:, 1, a:z], MULT
+            )
+            if i == 0:
+                nc.vector.tensor_add(v1[:], u1[:], q1[:])
+        for a, z in halves:
+            o = keep.tile([P, V // 2], F32, name=f"o1_{a}")
+            nc.vector.tensor_add(o[:], v1[:, a:z], z_t[1][:, 7, a:z])
+            nc.sync.dma_start(out=out[P : 2 * P, a:z], in_=o[:])

@@ -41,19 +41,20 @@ def tile_picked_agg_lin_none_sub_l_kernel(
             nc.sync.dma_start(out=raw[:], in_=x_view[:, c, :, a:z])
             x_raw.append((c, a, raw))
 
-        load_w(0)
         load_x(0, 0, T)
+        load_w(0)
         load_x(1, 0, 384)
         load_x(1, 384, T)
 
         gate_view = gate.rearrange("d (b p) v -> p b d v", p=P)
-        gates = [[], []]
+        gates = {}
         offs = []
 
-        def load_gate(b, pair):
-            g = keep.tile([P, 2, V], F32, name=f"gate{b}_{pair}")
-            nc.sync.dma_start(out=g[:], in_=gate_view[:, b, 2 * pair : 2 * pair + 2])
-            gates[b].append(g)
+        def load_gate(b, a, z):
+            g = keep.tile([P, z - a, V], F32, name=f"gate{b}_{a}")
+            nc.sync.dma_start(out=g[:], in_=gate_view[:, b, a:z])
+            for d in range(a, z):
+                gates[b, d] = g[:, d - a, :]
 
         def load_list():
             d = len(offs)
@@ -61,14 +62,14 @@ def tile_picked_agg_lin_none_sub_l_kernel(
             nc.sync.dma_start(o[:], lists[d])
             offs.append(o)
 
-        for pair in range(D // 2):
+        for d in range(0, D, 2):
             load_list()
-            load_gate(0, pair)
+            load_gate(0, d, d + 2)
             load_list()
-            if pair == 1:
+            if d == 2:
                 load_w(1)
-        for pair in range(D // 2):
-            load_gate(1, pair)
+        for d in range(0, D, 4):
+            load_gate(1, d, d + 4)
 
         def interleave(dst, src, v_cols):
             cols = dst.shape[1]
@@ -111,8 +112,8 @@ def tile_picked_agg_lin_none_sub_l_kernel(
             interleave(x_grp[c][:, a:z, :], raw[:, :, a - first : z - first], v_cols)
             quantise(x_codes[c][:, a:z], x_scales[c][:, a:z], x_grp[c][:, a:z, :])
 
+        prepare_x(0, 0, T, x_raw[0][2], 0, 288)
         prepare_w(0, 80)
-        prepare_x(0, 0, T, x_raw[0][2], 0, 320)
         spans = ((0, 256), (256, 384), (384, 512))
         acc0 = [psum.tile([P, z - a], F32, name=f"acc0_{a}") for a, z in spans]
         acc1 = psum.tile([P, T], F32, name="acc1")
@@ -120,59 +121,43 @@ def tile_picked_agg_lin_none_sub_l_kernel(
             multiply(acc0[i], 0, 0, a, z)
 
         y = [keep.tile([P, T], F32, name=f"y{b}") for b in range(2)]
+        v_cols = (160, 80, 96)
         for i, (a, z) in enumerate(spans):
             c_in, first, raw = x_raw[1] if z <= 384 else x_raw[2]
-            prepare_x(1, a, z, raw, first, (z - a) * 5 // 8)
+            prepare_x(1, a, z, raw, first, v_cols[i])
             multiply(acc0[i], 0, 1, a, z)
             nc.scalar.copy(out=y[0][:, a:z], in_=acc0[i][:])
 
-        z_t = [keep.tile([P, D, V], F32, name=f"z{b}") for b in range(2)]
+        z_t = keep.tile([P, D, 2, V], F32, name="z")
 
         def gather(b, d):
-            nc.vector.tensor_tensor(
-                z_t[b][:, d, :], y[b][:].indirect(offs[d][:]), gates[b][d // 2][:, d % 2, :], MULT
-            )
+            nc.vector.tensor_tensor(z_t[:, d, b, :], y[b][:].indirect(offs[d][:]), gates[b, d], MULT)
 
-        s0 = [keep.tile([P, 2, V], F32, name=f"s0_{i}") for i in range(3)]
-        o0 = keep.tile([P, V], F32, name="o0")
+        s1 = keep.tile([P, 2, 2, V], F32, name="s1")
+        s2 = keep.tile([P, 2, 2, V], F32, name="s2")
+        s3 = keep.tile([P, 2, V], F32, name="s3")
+        c0 = keep.tile([P, V], F32, name="c0")
+        e1 = keep.tile([P, V], F32, name="e1")
+        o = [keep.tile([P, V], F32, name=f"o{b}") for b in range(2)]
         for d in range(5):
             gather(0, d)
-        nc.vector.tensor_add(s0[0][:], z_t[0][:, 0:2], z_t[0][:, 2:4])
-        gather(0, 5)
         prepare_w(1, 0)
         for c in range(PASSES):
             multiply(acc1, 1, c, 0, T)
         nc.scalar.copy(out=y[1][:], in_=acc1[:])
-        gather(0, 6)
-        nc.vector.tensor_add(s0[1][:], s0[0][:], z_t[0][:, 4:6])
-        gather(0, 7)
-        gather(1, 0)
-        nc.vector.tensor_add(s0[2][:], s0[1][:], z_t[0][:, 6:8])
-        gather(1, 1)
-        nc.vector.tensor_add(o0[:], s0[2][:, 0], s0[2][:, 1])
-        nc.sync.dma_start(out=out[0:P, :], in_=o0[:])
-
-        s1 = keep.tile([P, 2, V], F32, name="s1")
-        t1 = keep.tile([P, V], F32, name="t1")
-        u1 = keep.tile([P, V], F32, name="u1")
-        q1 = keep.tile([P, V], F32, name="q1")
-        v1 = keep.tile([P, V], F32, name="v1")
-        for d in range(2, 5):
+        for d in range(5, D):
+            gather(0, d)
+        for d in range(5):
             gather(1, d)
-        nc.vector.tensor_add(s1[:], z_t[1][:, 0:2], z_t[1][:, 2:4])
+        nc.vector.tensor_add(s1[:], z_t[:, 0:2], z_t[:, 2:4])
         gather(1, 5)
-        nc.vector.tensor_add(t1[:], s1[:, 0], s1[:, 1])
+        nc.vector.tensor_add(c0[:], z_t[:, 6, 0], z_t[:, 7, 0])
+        nc.vector.tensor_add(s2[:], s1[:], z_t[:, 4:6])
         gather(1, 6)
-        nc.vector.tensor_add(u1[:], z_t[1][:, 4], z_t[1][:, 5])
-        nc.vector.tensor_add(q1[:], t1[:], z_t[1][:, 6])
-        halves = [(0, V // 2), (V // 2, V)]
-        for i, (a, z) in enumerate(halves):
-            nc.vector.tensor_tensor(
-                z_t[1][:, 7, a:z], y[1][:].indirect(offs[7][:, a // 16 : z // 16]), gates[1][3][:, 1, a:z], MULT
-            )
-            if i == 0:
-                nc.vector.tensor_add(v1[:], u1[:], q1[:])
-        for a, z in halves:
-            o = keep.tile([P, V // 2], F32, name=f"o1_{a}")
-            nc.vector.tensor_add(o[:], v1[:, a:z], z_t[1][:, 7, a:z])
-            nc.sync.dma_start(out=out[P : 2 * P, a:z], in_=o[:])
+        nc.vector.tensor_add(s3[:], s2[:, 0], s2[:, 1])
+        gather(1, 7)
+        nc.vector.tensor_add(e1[:], s3[:, 1], z_t[:, 6, 1])
+        nc.vector.tensor_add(o[0][:], s3[:, 0], c0[:])
+        nc.sync.dma_start(out=out[0:P, :], in_=o[0][:])
+        nc.vector.tensor_add(o[1][:], e1[:], z_t[:, 7, 1])
+        nc.sync.dma_start(out=out[P : 2 * P, :], in_=o[1][:])

@@ -1,10 +1,13 @@
 import concourse.mybir as mybir
+from concourse.masks import make_identity
 from contextlib import ExitStack
 
 K, T, N, D, V = 1024, 512, 256, 8, 256
 P, PACK = 128, 4
 PASSES = K // (P * PACK)
 FLOPS = 2 * K * T * N + 2 * D * N * V
+HALF = T // 2
+GROWS = P // D
 
 F32 = mybir.dt.float32
 BF16 = mybir.dt.bfloat16
@@ -13,6 +16,8 @@ U16 = mybir.dt.uint16
 U8 = mybir.dt.uint8
 FP8X4 = mybir.dt.float8_e4m3fn_x4
 MULT = mybir.AluOpType.mult
+ADD = mybir.AluOpType.add
+COPY = mybir.ActivationFunctionType.Copy
 
 
 def tile_picked_agg_lin_none_sub_l_kernel(
@@ -23,141 +28,177 @@ def tile_picked_agg_lin_none_sub_l_kernel(
     with ExitStack() as ctx:
         keep = ctx.enter_context(tc.tile_pool(name="keep", bufs=1))
         psum = ctx.enter_context(tc.psum_pool(name="psum", bufs=1))
+        turn = ctx.enter_context(tc.psum_pool(name="turn", bufs=4))
 
         w_view = w.rearrange("(c p j) n -> p c j n", c=PASSES, j=PACK)
         x_view = xT.rearrange("(c p j) t -> p c j t", c=PASSES, j=PACK)
-        w_raw = [[], []]
-
-        def load_w(b):
-            for c in range(PASSES):
-                raw = keep.tile([P, PACK, P], F32, name=f"w_raw{b}_{c}")
-                nc.sync.dma_start(out=raw[:], in_=w_view[:, c, :, b * P : (b + 1) * P])
-                w_raw[b].append(raw)
-
         x_raw = []
-
-        def load_x(c, a, z):
-            raw = keep.tile([P, PACK, z - a], F32, name=f"x_raw{c}_{a}")
-            nc.sync.dma_start(out=raw[:], in_=x_view[:, c, :, a:z])
-            x_raw.append((c, a, raw))
-
-        load_x(0, 0, T)
-        load_w(0)
-        load_x(1, 0, 384)
-        load_x(1, 384, T)
-
-        gate_view = gate.rearrange("d (b p) v -> p b d v", p=P)
-        gates = {}
+        w_raw = []
+        for c in range(PASSES):
+            raw = keep.tile([P, PACK, T], F32, name=f"x_raw{c}")
+            nc.sync.dma_start(out=raw[:], in_=x_view[:, c])
+            x_raw.append(raw)
+            raw = keep.tile([P, PACK, N], F32, name=f"w_raw{c}")
+            nc.sync.dma_start(out=raw[:], in_=w_view[:, c])
+            w_raw.append(raw)
         offs = []
 
-        def load_gate(b, a, z):
-            g = keep.tile([P, z - a, V], F32, name=f"gate{b}_{a}")
-            nc.sync.dma_start(out=g[:], in_=gate_view[:, b, a:z])
-            for d in range(a, z):
-                gates[b, d] = g[:, d - a, :]
-
         def load_list():
-            d = len(offs)
-            o = keep.tile([P, V // 16], U16, name=f"offs{d}")
-            nc.sync.dma_start(o[:], lists[d])
+            o = keep.tile([P, V // 16], U16, name=f"offs{len(offs)}")
+            nc.sync.dma_start(o[:], lists[len(offs)])
             offs.append(o)
 
-        for d in range(0, D, 2):
+        load_list()
+        gate_rows = keep.tile([P, V], F32, name="gate_rows")
+        nc.sync.dma_start(out=gate_rows[:], in_=gate.rearrange("d (a r) v -> (d a) r v", a=GROWS)[:, 0, :])
+        for d in range(1, D):
             load_list()
-            load_gate(0, d, d + 2)
-            load_list()
-            if d == 2:
-                load_w(1)
-        for d in range(0, D, 4):
-            load_gate(1, d, d + 4)
+
+        ident = keep.tile([P, P], F32, name="ident")
+        make_identity(nc, ident[:])
 
         def interleave(dst, src, v_cols):
             cols = dst.shape[1]
             if v_cols > 0:
-                nc.vector.tensor_copy(out=dst[:, 0:v_cols, :], in_=src[:, :, 0:v_cols].rearrange("p j w -> p w j"))
+                nc.vector.tensor_copy(
+                    out=dst[:, 0:v_cols, :].rearrange("p (c i) j -> p c j i", i=4),
+                    in_=src[:, :, 0:v_cols].rearrange("p j (c i) -> p c j i", i=4),
+                )
             if v_cols < cols:
-                nc.scalar.copy(out=dst[:, v_cols:cols, :], in_=src[:, :, v_cols:cols].rearrange("p j w -> p w j"))
+                nc.scalar.copy(
+                    out=dst[:, v_cols:cols, :].rearrange("p (c i) j -> p c j i", i=4),
+                    in_=src[:, :, v_cols:cols].rearrange("p j (c i) -> p c j i", i=4),
+                )
 
         def quantise(codes, scales, grouped):
             nc.vector.quantize_mx(
                 out=codes.bitcast(FP8X4), scales=scales, in_=grouped.rearrange("p n j -> p (n j)")
             )
 
-        w_codes = [keep.tile([P, PASSES, P], U32, name=f"w_codes{b}", align_bytes=64) for b in range(2)]
-        w_scales = [keep.tile([P, PASSES, P], U8, name=f"w_scales{b}", align_bytes=64) for b in range(2)]
-        w_grp = [keep.tile([P, PASSES * P, PACK], BF16, name=f"w_grp{b}", align_bytes=64) for b in range(2)]
+        w_codes = [keep.tile([P, N], U32, name=f"w_codes{c}", align_bytes=64) for c in range(PASSES)]
+        w_scales = [keep.tile([P, N], U8, name=f"w_scales{c}", align_bytes=64) for c in range(PASSES)]
+        w_grp = [keep.tile([P, N, PACK], BF16, name=f"w_grp{c}", align_bytes=64) for c in range(PASSES)]
         x_codes = [keep.tile([P, T], U32, name=f"x_codes{c}", align_bytes=64) for c in range(PASSES)]
         x_scales = [keep.tile([P, T], U8, name=f"x_scales{c}", align_bytes=64) for c in range(PASSES)]
         x_grp = [keep.tile([P, T, PACK], BF16, name=f"x_grp{c}", align_bytes=64) for c in range(PASSES)]
+        acc = [[psum.tile([P, HALF], F32, name=f"acc{b}_{h}") for h in range(2)] for b in range(2)]
+        y = [keep.tile([P, T], F32, name=f"y{b}") for b in range(2)]
 
-        def prepare_w(b, v_cols):
-            for c in range(PASSES):
-                interleave(w_grp[b][:, c * P : (c + 1) * P, :], w_raw[b][c][:], v_cols)
-            quantise(
-                w_codes[b][:].rearrange("p c n -> p (c n)"), w_scales[b][:].rearrange("p c n -> p (c n)"), w_grp[b][:]
-            )
+        def quantise_w(c, a, z):
+            quantise(w_codes[c][:, a:z], w_scales[c][:, a:z], w_grp[c][:, a:z, :])
 
-        def multiply(acc, b, c, a, z):
+        def quantise_x(c, a, z):
+            quantise(x_codes[c][:, a:z], x_scales[c][:, a:z], x_grp[c][:, a:z, :])
+
+        def multiply(b, h, c):
+            nodes = slice(h * HALF, (h + 1) * HALF)
+            cols = slice(b * P, (b + 1) * P)
             nc.tensor.matmul_mx(
-                out=acc[:],
-                lhsT=w_codes[b][:, c, :].bitcast(FP8X4),
-                lhsT_scale=w_scales[b][:, c, :],
-                rhs=x_codes[c][:, a:z].bitcast(FP8X4),
-                rhs_scale=x_scales[c][:, a:z],
+                out=acc[b][h][:],
+                lhsT=w_codes[c][:, cols].bitcast(FP8X4),
+                lhsT_scale=w_scales[c][:, cols],
+                rhs=x_codes[c][:, nodes].bitcast(FP8X4),
+                rhs_scale=x_scales[c][:, nodes],
                 start=(c == 0),
                 stop=(c == PASSES - 1),
             )
 
-        def prepare_x(c, a, z, raw, first, v_cols):
-            interleave(x_grp[c][:, a:z, :], raw[:, :, a - first : z - first], v_cols)
-            quantise(x_codes[c][:, a:z], x_scales[c][:, a:z], x_grp[c][:, a:z, :])
+        interleave(x_grp[0][:], x_raw[0][:], 288)
+        quantise_x(0, 0, T)
+        interleave(w_grp[0][:], w_raw[0][:], 160)
+        quantise_w(0, 0, N)
+        for b in range(2):
+            for h in range(2):
+                multiply(b, h, 0)
+        interleave(x_grp[1][:], x_raw[1][:], 288)
+        quantise_x(1, 0, HALF)
+        interleave(w_grp[1][:, 0:P, :], w_raw[1][:, :, 0:P], 64)
+        quantise_x(1, HALF, T)
+        quantise_w(1, 0, P)
+        interleave(w_grp[1][:, P:N, :], w_raw[1][:, :, P:N], 0)
+        for h in range(2):
+            multiply(0, h, 1)
+        nc.vector.tensor_copy(out=y[0][:, 0:HALF], in_=acc[0][0][:])
+        nc.scalar.copy(out=y[0][:, HALF:T], in_=acc[0][1][:])
+        quantise_w(1, P, N)
+        for h in range(2):
+            multiply(1, h, 1)
+            nc.scalar.copy(out=y[1][:, h * HALF : (h + 1) * HALF], in_=acc[1][h][:])
 
-        prepare_x(0, 0, T, x_raw[0][2], 0, 288)
-        prepare_w(0, 80)
-        spans = ((0, 256), (256, 384), (384, 512))
-        acc0 = [psum.tile([P, z - a], F32, name=f"acc0_{a}") for a, z in spans]
-        acc1 = psum.tile([P, T], F32, name="acc1")
-        for i, (a, z) in enumerate(spans):
-            multiply(acc0[i], 0, 0, a, z)
+        gate_t = keep.tile([P, 2, D], F32, name="gate_t")
+        gt = turn.tile([P, 2, P], F32, name="gt", tag="turned")
+        for h in range(2):
+            nc.tensor.transpose(gt[:, h, :], gate_rows[:, h * P : (h + 1) * P], ident[:])
+        nc.scalar.copy(out=gate_t[:], in_=gt[:].rearrange("p h (d a) -> p h d a", a=GROWS)[:, :, :, 0])
 
-        y = [keep.tile([P, T], F32, name=f"y{b}") for b in range(2)]
-        v_cols = (160, 80, 96)
-        for i, (a, z) in enumerate(spans):
-            c_in, first, raw = x_raw[1] if z <= 384 else x_raw[2]
-            prepare_x(1, a, z, raw, first, v_cols[i])
-            multiply(acc0[i], 0, 1, a, z)
-            nc.scalar.copy(out=y[0][:, a:z], in_=acc0[i][:])
+        z_t = [keep.tile([P, 2, V], F32, name=f"z{d}") for d in range(D)]
+        zt = []
 
-        z_t = keep.tile([P, D, 2, V], F32, name="z")
+        def gather(d, b):
+            nc.vector.tensor_copy(z_t[d][:, b, :], y[b][:].indirect(offs[d][:]))
 
-        def gather(b, d):
-            nc.vector.tensor_tensor(z_t[:, d, b, :], y[b][:].indirect(offs[d][:]), gates[b, d], MULT)
+        def turn_over(d):
+            t = turn.tile([P, 2, 2, P], F32, name=f"zt{d}", tag="turned")
+            for b in range(2):
+                for h in range(2):
+                    nc.tensor.transpose(t[:, h, b, :], z_t[d][:, b, h * P : (h + 1) * P], ident[:])
+            return t
 
-        s1 = keep.tile([P, 2, 2, V], F32, name="s1")
-        s2 = keep.tile([P, 2, 2, V], F32, name="s2")
-        s3 = keep.tile([P, 2, V], F32, name="s3")
-        c0 = keep.tile([P, V], F32, name="c0")
-        e1 = keep.tile([P, V], F32, name="e1")
-        o = [keep.tile([P, V], F32, name=f"o{b}") for b in range(2)]
-        for d in range(5):
-            gather(0, d)
-        prepare_w(1, 0)
-        for c in range(PASSES):
-            multiply(acc1, 1, c, 0, T)
-        nc.scalar.copy(out=y[1][:], in_=acc1[:])
-        for d in range(5, D):
-            gather(0, d)
-        for d in range(5):
-            gather(1, d)
-        nc.vector.tensor_add(s1[:], z_t[:, 0:2], z_t[:, 2:4])
-        gather(1, 5)
-        nc.vector.tensor_add(c0[:], z_t[:, 6, 0], z_t[:, 7, 0])
-        nc.vector.tensor_add(s2[:], s1[:], z_t[:, 4:6])
-        gather(1, 6)
-        nc.vector.tensor_add(s3[:], s2[:, 0], s2[:, 1])
-        gather(1, 7)
-        nc.vector.tensor_add(e1[:], s3[:, 1], z_t[:, 6, 1])
-        nc.vector.tensor_add(o[0][:], s3[:, 0], c0[:])
-        nc.sync.dma_start(out=out[0:P, :], in_=o[0][:])
-        nc.vector.tensor_add(o[1][:], e1[:], z_t[:, 7, 1])
-        nc.sync.dma_start(out=out[P : 2 * P, :], in_=o[1][:])
+        def weigh(d, t):
+            zg = keep.tile([P, 2, 2, P], F32, name=f"zg{d}")
+            for h in range(2):
+                nc.scalar.activation(out=zg[:, h], in_=t[:, h], func=COPY, scale=gate_t[:, h, d : d + 1])
+            return zg
+
+        def add_on_gpsimd(d, left, right):
+            r = keep.tile([P, 2, 2, P], F32, name=f"r{d}")
+            nc.gpsimd.tensor_tensor(out=r[:], in0=left[:], in1=right[:], op=ADD)
+            return r
+
+        def weigh_and_add(d, t, left, r, h, b):
+            nc.vector.scalar_tensor_tensor(
+                out=r[:, h, b], in0=t[:, h, b], scalar=gate_t[:, h, d : d + 1], in1=left[:, h, b], op0=MULT, op1=ADD
+            )
+
+        for b in range(2):
+            for d in range(2):
+                gather(d, b)
+        total = weigh(0, turn_over(0))
+        total = add_on_gpsimd(1, total, weigh(1, turn_over(1)))
+        for d in range(2, D - 3):
+            for b in range(2):
+                gather(d, b)
+            total = add_on_gpsimd(d, total, weigh(d, turn_over(d)))
+        turned = {}
+        for d in range(D - 3, D - 1):
+            for b in range(2):
+                gather(d, b)
+            turned[d] = turn_over(d)
+        for b in range(2):
+            gather(D - 1, b)
+            if b < 3 - 1:
+                d = D - 3 + b
+                r = keep.tile([P, 2, 2, P], F32, name=f"r{d}")
+                for h in range(2):
+                    weigh_and_add(d, turned[d], total, r, h, slice(0, 2))
+                total = r
+        turned[D - 1] = turn_over(D - 1)
+        r = keep.tile([P, 2, 2, P], F32, name=f"r{D - 1}")
+        for b in range(2):
+            for h in range(2):
+                weigh_and_add(D - 1, turned[D - 1], total, r, h, b)
+        o0 = keep.tile([P, 2, P], F32, name="o0")
+        ot0 = turn.tile([P, 2, P], F32, name="ot0", tag="turned")
+        for h in range(2):
+            nc.tensor.transpose(ot0[:, h], r[:, h, 0], ident[:])
+        nc.scalar.copy(out=o0[:], in_=ot0[:])
+        nc.sync.dma_start(out=out[0:P, :], in_=o0[:].rearrange("p h v -> p (h v)"))
+        for h in range(2):
+            ot = turn.tile([P, P], F32, name=f"ot1_{h}", tag="turned")
+            nc.tensor.transpose(ot[:], r[:, h, 1], ident[:])
+            o = keep.tile([P, P], F32, name=f"o1_{h}")
+            if h == 0:
+                nc.vector.tensor_copy(out=o[:], in_=ot[:])
+            else:
+                nc.scalar.copy(out=o[:], in_=ot[:])
+            nc.sync.dma_start(out=out[P : 2 * P, h * P : (h + 1) * P], in_=o[:])

import concourse.mybir as mybir
from concourse.masks import make_identity
from contextlib import ExitStack

K, T, N, D, V = 1024, 512, 256, 8, 256
P, PACK = 128, 4
PASSES = K // (P * PACK)
FLOPS = 2 * K * T * N + 2 * D * N * V
HALF = T // 2
GROWS = P // D

F32 = mybir.dt.float32
BF16 = mybir.dt.bfloat16
U32 = mybir.dt.uint32
U16 = mybir.dt.uint16
U8 = mybir.dt.uint8
FP8X4 = mybir.dt.float8_e4m3fn_x4
MULT = mybir.AluOpType.mult
ADD = mybir.AluOpType.add
COPY = mybir.ActivationFunctionType.Copy


def tile_picked_agg_lin_none_sub_l_kernel(
    tc, xT, w, gate, pos1, pos2, pos3, pos4, pos5, pos6, pos7, pos8, out
):
    nc = tc.nc
    lists = (pos1, pos2, pos3, pos4, pos5, pos6, pos7, pos8)
    with ExitStack() as ctx:
        keep = ctx.enter_context(tc.tile_pool(name="keep", bufs=1))
        psum = ctx.enter_context(tc.psum_pool(name="psum", bufs=1))
        turn = ctx.enter_context(tc.psum_pool(name="turn", bufs=4))

        w_view = w.rearrange("(c p j) n -> p c j n", c=PASSES, j=PACK)
        x_view = xT.rearrange("(c p j) t -> p c j t", c=PASSES, j=PACK)
        x_raw = []
        w_raw = []
        for c in range(PASSES):
            raw = keep.tile([P, PACK, T], F32, name=f"x_raw{c}")
            nc.sync.dma_start(out=raw[:], in_=x_view[:, c])
            x_raw.append(raw)
            raw = keep.tile([P, PACK, N], F32, name=f"w_raw{c}")
            nc.sync.dma_start(out=raw[:], in_=w_view[:, c])
            w_raw.append(raw)
        offs = []

        def load_list():
            o = keep.tile([P, V // 16], U16, name=f"offs{len(offs)}")
            nc.sync.dma_start(o[:], lists[len(offs)])
            offs.append(o)

        load_list()
        gate_rows = keep.tile([P, V], F32, name="gate_rows")
        nc.sync.dma_start(out=gate_rows[:], in_=gate.rearrange("d (a r) v -> (d a) r v", a=GROWS)[:, 0, :])
        for d in range(1, D):
            load_list()

        ident = keep.tile([P, P], F32, name="ident")
        make_identity(nc, ident[:])

        def interleave(dst, src, v_cols):
            cols = dst.shape[1]
            if v_cols > 0:
                nc.vector.tensor_copy(
                    out=dst[:, 0:v_cols, :].rearrange("p (c i) j -> p c j i", i=4),
                    in_=src[:, :, 0:v_cols].rearrange("p j (c i) -> p c j i", i=4),
                )
            if v_cols < cols:
                nc.scalar.copy(
                    out=dst[:, v_cols:cols, :].rearrange("p (c i) j -> p c j i", i=4),
                    in_=src[:, :, v_cols:cols].rearrange("p j (c i) -> p c j i", i=4),
                )

        def quantise(codes, scales, grouped):
            nc.vector.quantize_mx(
                out=codes.bitcast(FP8X4), scales=scales, in_=grouped.rearrange("p n j -> p (n j)")
            )

        w_codes = [keep.tile([P, N], U32, name=f"w_codes{c}", align_bytes=64) for c in range(PASSES)]
        w_scales = [keep.tile([P, N], U8, name=f"w_scales{c}", align_bytes=64) for c in range(PASSES)]
        w_grp = [keep.tile([P, N, PACK], BF16, name=f"w_grp{c}", align_bytes=64) for c in range(PASSES)]
        x_codes = [keep.tile([P, T], U32, name=f"x_codes{c}", align_bytes=64) for c in range(PASSES)]
        x_scales = [keep.tile([P, T], U8, name=f"x_scales{c}", align_bytes=64) for c in range(PASSES)]
        x_grp = [keep.tile([P, T, PACK], BF16, name=f"x_grp{c}", align_bytes=64) for c in range(PASSES)]
        acc = [[psum.tile([P, HALF], F32, name=f"acc{b}_{h}") for h in range(2)] for b in range(2)]
        y = [keep.tile([P, T], F32, name=f"y{b}") for b in range(2)]

        def quantise_w(c, a, z):
            quantise(w_codes[c][:, a:z], w_scales[c][:, a:z], w_grp[c][:, a:z, :])

        def quantise_x(c, a, z):
            quantise(x_codes[c][:, a:z], x_scales[c][:, a:z], x_grp[c][:, a:z, :])

        def multiply(b, h, c):
            nodes = slice(h * HALF, (h + 1) * HALF)
            cols = slice(b * P, (b + 1) * P)
            nc.tensor.matmul_mx(
                out=acc[b][h][:],
                lhsT=w_codes[c][:, cols].bitcast(FP8X4),
                lhsT_scale=w_scales[c][:, cols],
                rhs=x_codes[c][:, nodes].bitcast(FP8X4),
                rhs_scale=x_scales[c][:, nodes],
                start=(c == 0),
                stop=(c == PASSES - 1),
            )

        interleave(x_grp[0][:], x_raw[0][:], 288)
        quantise_x(0, 0, T)
        interleave(w_grp[0][:], w_raw[0][:], 160)
        quantise_w(0, 0, N)
        for b in range(2):
            for h in range(2):
                multiply(b, h, 0)
        interleave(x_grp[1][:], x_raw[1][:], 288)
        quantise_x(1, 0, HALF)
        interleave(w_grp[1][:, 0:P, :], w_raw[1][:, :, 0:P], 64)
        quantise_x(1, HALF, T)
        quantise_w(1, 0, P)
        interleave(w_grp[1][:, P:N, :], w_raw[1][:, :, P:N], 0)
        for h in range(2):
            multiply(0, h, 1)
        nc.vector.tensor_copy(out=y[0][:, 0:HALF], in_=acc[0][0][:])
        nc.scalar.copy(out=y[0][:, HALF:T], in_=acc[0][1][:])
        quantise_w(1, P, N)
        for h in range(2):
            multiply(1, h, 1)
            nc.scalar.copy(out=y[1][:, h * HALF : (h + 1) * HALF], in_=acc[1][h][:])

        gate_t = keep.tile([P, 2, D], F32, name="gate_t")
        gt = turn.tile([P, 2, P], F32, name="gt", tag="turned")
        for h in range(2):
            nc.tensor.transpose(gt[:, h, :], gate_rows[:, h * P : (h + 1) * P], ident[:])
        nc.scalar.copy(out=gate_t[:], in_=gt[:].rearrange("p h (d a) -> p h d a", a=GROWS)[:, :, :, 0])

        z_t = [keep.tile([P, 2, V], F32, name=f"z{d}") for d in range(D)]
        zt = []

        def gather(d, b):
            nc.vector.tensor_copy(z_t[d][:, b, :], y[b][:].indirect(offs[d][:]))

        def turn_over(d):
            t = turn.tile([P, 2, 2, P], F32, name=f"zt{d}", tag="turned")
            for b in range(2):
                for h in range(2):
                    nc.tensor.transpose(t[:, h, b, :], z_t[d][:, b, h * P : (h + 1) * P], ident[:])
            return t

        def weigh(d, t):
            zg = keep.tile([P, 2, 2, P], F32, name=f"zg{d}")
            for h in range(2):
                nc.scalar.activation(out=zg[:, h], in_=t[:, h], func=COPY, scale=gate_t[:, h, d : d + 1])
            return zg

        def add_on_gpsimd(d, left, right):
            r = keep.tile([P, 2, 2, P], F32, name=f"r{d}")
            nc.gpsimd.tensor_tensor(out=r[:], in0=left[:], in1=right[:], op=ADD)
            return r

        def weigh_and_add(d, t, left, r, h, b):
            nc.vector.scalar_tensor_tensor(
                out=r[:, h, b], in0=t[:, h, b], scalar=gate_t[:, h, d : d + 1], in1=left[:, h, b], op0=MULT, op1=ADD
            )

        for b in range(2):
            for d in range(2):
                gather(d, b)
        total = weigh(0, turn_over(0))
        total = add_on_gpsimd(1, total, weigh(1, turn_over(1)))
        for d in range(2, D - 3):
            for b in range(2):
                gather(d, b)
            total = add_on_gpsimd(d, total, weigh(d, turn_over(d)))
        turned = {}
        for d in range(D - 3, D - 1):
            for b in range(2):
                gather(d, b)
            turned[d] = turn_over(d)
        for b in range(2):
            gather(D - 1, b)
            if b < 3 - 1:
                d = D - 3 + b
                r = keep.tile([P, 2, 2, P], F32, name=f"r{d}")
                for h in range(2):
                    weigh_and_add(d, turned[d], total, r, h, slice(0, 2))
                total = r
        turned[D - 1] = turn_over(D - 1)
        r = keep.tile([P, 2, 2, P], F32, name=f"r{D - 1}")
        for b in range(2):
            for h in range(2):
                weigh_and_add(D - 1, turned[D - 1], total, r, h, b)
        o0 = keep.tile([P, 2, P], F32, name="o0")
        ot0 = turn.tile([P, 2, P], F32, name="ot0", tag="turned")
        for h in range(2):
            nc.tensor.transpose(ot0[:, h], r[:, h, 0], ident[:])
        nc.scalar.copy(out=o0[:], in_=ot0[:])
        nc.sync.dma_start(out=out[0:P, :], in_=o0[:].rearrange("p h v -> p (h v)"))
        for h in range(2):
            ot = turn.tile([P, P], F32, name=f"ot1_{h}", tag="turned")
            nc.tensor.transpose(ot[:], r[:, h, 1], ident[:])
            o = keep.tile([P, P], F32, name=f"o1_{h}")
            if h == 0:
                nc.vector.tensor_copy(out=o[:], in_=ot[:])
            else:
                nc.scalar.copy(out=o[:], in_=ot[:])
            nc.sync.dma_start(out=out[P : 2 * P, h * P : (h + 1) * P], in_=o[:])
